import numpy as np
import ml_dtypes


def mxq(x, axis, fmt="e4m3"):
    dtype, down = {"e4m3": (ml_dtypes.float8_e4m3fn, 7), "e5m2": (ml_dtypes.float8_e5m2, 14)}[fmt]
    v = np.moveaxis(np.asarray(x, np.float32).astype(ml_dtypes.bfloat16).astype(np.float64), axis, -1)
    blocks = v.reshape(v.shape[:-1] + (-1, 32))
    amax = np.abs(blocks).max(-1, keepdims=True)
    byte = np.maximum(np.where(amax > 0, np.frexp(amax)[1] - 1 + 127, 0) - down, 1)
    scale = np.exp2(byte - 127.0)
    codes = (blocks / scale).astype(np.float32).astype(dtype).astype(np.float64)
    return np.moveaxis((codes * scale).reshape(v.shape), -1, axis)


WIDE = False


def mx_kscale(k):
    if not WIDE:
        return np.ones(k)
    levels = np.array([10, -10, 5, -5, 0])
    if k % 512:
        return np.exp2(np.random.permutation(np.resize(levels, k // 32))).repeat(32)
    a = np.empty((k // 512, 16))
    for p in range(k // 512):
        a[p, :8] = np.random.permutation(np.resize(levels, 8))
        for g in range(8):
            far = levels[np.abs(levels - a[p, g]) >= 10]
            a[p, g + 8] = far[np.random.randint(len(far))]
    return np.exp2(a.ravel()).repeat(32)


BF16 = ml_dtypes.bfloat16


def bf(x):
    return np.asarray(x, np.float32).astype(BF16)


def f64(x):
    return np.asarray(x).astype(np.float64)


E2M1 = np.array([0.0, 0.5, 1.0, 1.5, 2.0, 3.0, 4.0, 6.0, -0.0, -0.5, -1.0, -1.5, -2.0, -3.0, -4.0, -6.0])


def pack_weight(w, fmt):
    k, n = w.shape
    w = f64(bf(w)).reshape(k // 32, 32, n)
    amax = np.abs(w).max(1)
    if fmt == "e4m3":
        byte = np.frexp(amax)[1] - 1 + 127 - 7
    else:
        mant, ex = np.frexp(amax / 6.0)
        byte = np.where(mant > 0.5, ex, ex - 1) + 127
    byte = np.clip(np.where(amax > 0, byte, 1), 1, 254)
    scaled = (w * np.exp2(127.0 - byte)[:, None, :]).reshape(k, n).astype(np.float32)
    by_word = np.ascontiguousarray(scaled.reshape(k // 512, 128, 4, n).transpose(0, 1, 3, 2))
    if fmt == "e4m3":
        words = by_word.astype(ml_dtypes.float8_e4m3fn).view(np.uint8)
    else:
        c = by_word.astype(ml_dtypes.float4_e2m1fn).view(np.uint8) & 0xF
        words = c[..., 0::2] | (c[..., 1::2] << 4)
    return np.ascontiguousarray(words), np.ascontiguousarray(byte.astype(np.uint8).reshape(k // 512, 16, n))


def unpack_weight(words, scales, fmt):
    g, p, n, _ = words.shape
    if fmt == "e4m3":
        vals = np.ascontiguousarray(words).view(ml_dtypes.float8_e4m3fn).astype(np.float64)
    else:
        nib = np.empty((g, p, n, 4), np.uint8)
        nib[..., 0::2] = words & 0xF
        nib[..., 1::2] = words >> 4
        vals = E2M1[nib]
    vals = vals * np.repeat(np.exp2(scales.astype(np.float64) - 127.0), 8, axis=1)[..., None]
    return vals.transpose(0, 1, 3, 2).reshape(g * 512, n)
def pack4(w):
    words, scales = pack_weight(w, "e2m1")
    return words.reshape(words.shape[0], 128, -1), scales


def unpack4(words, scales):
    return unpack_weight(words.reshape(words.shape[0], 128, -1, 2), scales, "e2m1")


def planes(Y):
    n, m = Y.shape
    b = f64(bf(Y)).reshape(n // 32, 32, m)
    amax = np.abs(b).max(1)
    byte = np.clip(np.where(amax > 0, np.frexp(amax)[1] - 1 + 127 - 7, 1), 1, 254)
    codes = (b * np.exp2(127.0 - byte)[:, None, :]).reshape(n, m).astype(np.float32).astype(ml_dtypes.float8_e4m3fn).view(np.uint8)
    words = codes.reshape(n // 512, 128, 4, m).transpose(0, 1, 3, 2)
    return np.ascontiguousarray(words), np.ascontiguousarray(byte.astype(np.uint8).reshape(n // 512, 16, m))


M, K, N = 768, 1536, 1024


def setup_inputs():
    s = mx_kscale(K)[:, None]
    spread = np.exp(0.8 * np.random.randn(1, N))
    xt = np.random.randn(K, M) * s
    u = 2.0 * spread * np.random.randn(K, N) / np.sqrt(K) / s
    w = 1.5 * np.random.randn(K, N) / np.sqrt(K) / s
    r = 1.2 * np.random.randn(K, N) / np.sqrt(K) / s
    x_words, x_scales = pack_weight(xt, "e4m3")
    u_words, u_scales = pack4(u)
    w_words, w_scales = pack_weight(w, "e4m3")
    return {"x_words": x_words, "x_scales": x_scales,
            "u_words": u_words, "u_scales": u_scales,
            "w_words": w_words, "w_scales": w_scales,
            "r": bf(r)}


def reference(x_words, x_scales, u_words, u_scales, w_words, w_scales, r):
    x = unpack_weight(x_words, x_scales, "e4m3").T
    u = unpack4(u_words, u_scales)
    w = unpack_weight(w_words, w_scales, "e4m3")
    rq = mxq(f64(r), 0, "e4m3")
    value = x @ u
    logit = x @ w
    resid = x @ rq
    gate = 1.0 / (1.0 + np.exp(-(logit - np.abs(resid))))
    y = value * gate
    words, scales = planes(y.T)
    return y, words, scales

@@ -1,0 +1,344 @@
+from contextlib import ExitStack
+
+import concourse.mybir as mybir
+from concourse.masks import make_identity
+
+M, K, N = 768, 1536, 1024
+FLOPS = 3 * 2 * M * K * N
+
+F32 = mybir.dt.float32
+BF16 = mybir.dt.bfloat16
+I32 = mybir.dt.int32
+U8 = mybir.dt.uint8
+FP8X4 = mybir.dt.float8_e4m3fn_x4
+FP4X4 = mybir.dt.float4_e2m1fn_x4
+ACT = mybir.ActivationFunctionType
+ALU = mybir.AluOpType
+
+P = 128
+PACK = 4
+SPAN = P * PACK
+PASSES = K // SPAN
+TILES = M // P
+HALVES = N // SPAN
+BANKS = 8
+W_ROW = 4
+
+
+def program_order():
+    steps = []
+    used = [0]
+
+    def bank():
+        used[0] += 1
+        return (used[0] - 1) % 8
+
+    def group(kind, h, j):
+        b = bank()
+        steps.extend(("mm", kind, h, j, g, b) for g in range(PASSES))
+
+    steps += [("load", "x", 0, (0,)), ("load", "u", 0, (0,)), ("clear", "x", "V"), ("clear", "u", "V"), ("clear", "w", "G")]
+    steps += [("setup",), ("scales", "x", "D"), ("scales", "u", "D"), ("scales", "w", "G")]
+    steps += [("load", "x", 0, (1,)), ("load", "u", 0, (1, 2)), ("load", "r", 0, (0,)), ("load", "x", 0, (2,))]
+    steps += [("load", "r", 0, (1,)), ("load", "r", 0, (2,)), ("load", "r", 1, (0,)), ("load", "r", 1, (1,))]
+    steps += [("load", "w", 0, (0, 1, 2)), ("load", "r", 1, (2,)), ("load", "w", 1, (0, 1, 2)), ("load", "u", 1, (0, 1, 2))]
+
+    banks = [bank() for j in range(TILES)]
+    for g in range(PASSES):
+        steps.extend(("mm", "u", 0, j, g, banks[j]) for j in range(TILES))
+    steps.extend(("keep_value", 0, j) for j in range(TILES))
+    for g in range(PASSES):
+        steps += [("weave", 0, g, "V", 0), ("weave", 0, g, "V", 1), ("quant_r", 0, g, 0), ("quant_r", 0, g, 1)]
+    steps += [("weave", 1, 0, "S")]
+    banks = [bank() for j in range(TILES)]
+    for g in range(PASSES):
+        steps.extend(("mm", "r", 0, j, g, banks[j]) for j in range(TILES))
+    steps.extend(("absolute", 0, j) for j in range(TILES))
+    steps += [("weave", 1, 1, "V"), ("quant_r", 1, 0), ("quant_r", 1, 1), ("weave", 1, 2, "V")]
+    for j in range(TILES):
+        group("w", 0, j)
+
+    def turn(*pairs):
+        steps.extend(("turn", h, js, bank()) for h, js in pairs)
+
+    def finish(h, js):
+        steps.extend([("unload", h, js, "S"), ("quant_y", h, js), ("store_words", h, js)])
+
+    def gate(h, j):
+        steps.extend([("margin", h, j), ("sigmoid", h, j)])
+
+    def result(h, j, engine):
+        steps.extend([("product", h, j), ("store_y", h, j), ("round", h, j, engine)])
+
+    def add(name, *args):
+        steps.append((name,) + args)
+
+    def product(h, j):
+        add("product", h, j)
+        add("store_y", h, j)
+
+    def planes(h, js):
+        add("quant_y", h, js)
+        add("store_words", h, js)
+
+    gate(0, 0)
+    add("quant_r", 1, 2)
+    gate(0, 1)
+    gate(0, 2)
+    product(0, 0)
+    gate(0, 3)
+    product(0, 1)
+    add("round", 0, 0, "S")
+    scalar_fill = {
+        0: [("sigmoid", 0, 4), ("sigmoid", 0, 5)],
+        1: [("round", 0, 2, "S")],
+        2: [("round", 0, 4, "S")],
+        3: [("unload", 0, (0, 1), "S"), ("unload", 0, (2, 3), "S")],
+        4: [("unload", 0, (4, 5), "S"), ("unload", 1, (0, 1), "S")],
+        5: [],
+    }
+    add("margin", 0, 4)
+    add("margin", 0, 5)
+    add("round", 0, 1, "V")
+    for j in range(TILES):
+        group("r", 1, j)
+        add("absolute", 1, j)
+        steps.extend(scalar_fill[j])
+        group("w", 1, j)
+        gate(1, j)
+        if j == 1:
+            add("round", 0, 3, "V")
+        if j > 0:
+            group("u", 1, j - 1)
+            product(1, j - 1)
+        if j == 0:
+            product(0, 2)
+        if j < 3:
+            product(0, j + 3)
+        if j == 3:
+            planes(0, (0, 1))
+        if j == 4:
+            planes(0, (4, 5))
+            add("store_scales", 0)
+        if 0 < j < 5:
+            add("round", 1, j - 1, "V")
+        if j == 2:
+            add("round", 0, 5, "V")
+        if j == 3:
+            planes(0, (2, 3))
+        if j == 4:
+            planes(1, (0, 1))
+        if j == 2:
+            turn((0, (0, 1)), (0, (2, 3)))
+        if j == 3:
+            turn((0, (4, 5)), (1, (0, 1)))
+    add("round", 1, 4, "S")
+    group("u", 1, 5)
+    add("product16", 1, 5)
+    product(1, 5)
+    turn((1, (2, 3)), (1, (4,)), (1, (5,)))
+    finish(1, (2, 3))
+    add("unload", 1, (4,), "S")
+    add("unload", 1, (5,), "V")
+    add("quant_y", 1, (4,))
+    add("quant_y", 1, (5,))
+    add("store_words", 1, (4, 5))
+    add("store_scales", 1)
+    return steps
+
+
+def tile_virtual_logit_gated_features_k3_kernel(
+    tc, x_words, x_scales, u_words, u_scales, w_words, w_scales, r, out_0, out_1, out_2
+):
+    nc = tc.nc
+    engines = {"V": nc.vector, "S": nc.scalar, "G": nc.gpsimd, "D": nc.sync}
+
+    with ExitStack() as ctx:
+        keep = ctx.enter_context(tc.tile_pool(name="keep", bufs=1))
+        psum = ctx.enter_context(tc.psum_pool(name="psum", bufs=1))
+
+        def sb(name, shape, dtype):
+            return keep.tile(shape, dtype, name=name, align_bytes=64)
+
+        banks = [psum.tile([P, SPAN], F32, name="bank%d" % b) for b in range(BANKS)]
+        x_codes = sb("x_codes", [P, PASSES, M], I32)
+        u_codes = [sb("u_codes%d" % h, [P, PASSES, 2 * SPAN], U8) for h in range(HALVES)]
+        w_codes = [sb("w_codes%d" % h, [P, PASSES, SPAN], I32) for h in range(HALVES)]
+        r_codes = [sb("r_codes%d" % h, [P, PASSES, SPAN], I32) for h in range(HALVES)]
+        r_plane = [sb("r_plane%d" % h, [P, PASSES, SPAN], U8) for h in range(HALVES)]
+        r_rows = [sb("r_rows%d" % h, [P, PASSES, PACK, SPAN], BF16) for h in range(HALVES)]
+        r_woven = [sb("r_woven%d" % h, [P, PASSES, SPAN * PACK], BF16) for h in range(HALVES)]
+        planes = {
+            "x": sb("x_plane", [P, PASSES, M], U8),
+            "u": sb("u_plane", [P, PASSES, N], U8),
+            "w": sb("w_plane", [P, PASSES, N], U8),
+        }
+        gate = [sb("gate%d" % h, [P, TILES, SPAN], F32) for h in range(HALVES)]
+        y32 = [sb("y32_%d" % h, [P, TILES, SPAN], F32) for h in range(HALVES)]
+        y16 = [sb("y16_%d" % h, [P, TILES, SPAN], BF16) for h in range(HALVES)]
+        y_turned = [sb("y_turned%d" % h, [P, M * PACK], BF16) for h in range(HALVES)]
+        y_codes = [sb("y_codes%d" % h, [P, M], I32) for h in range(HALVES)]
+        y_plane = [sb("y_plane%d" % h, [P, M], U8) for h in range(HALVES)]
+        ident = sb("ident", [P, P], F32)
+        one = sb("one", [P, 1], F32)
+        scale_rows = {"x": x_scales, "u": u_scales, "w": w_scales}
+        first_row = {"x": 0, "u": 0, "w": W_ROW}
+        bank_of = {}
+        kept = set()
+
+        def cols(h):
+            return slice(h * SPAN, (h + 1) * SPAN)
+
+        def rows(j):
+            return slice(j * P, (j + 1) * P)
+
+        def clear(kind, engine):
+            engines[engine].memset(planes[kind][:].rearrange("p g n -> p (g n)").bitcast(I32), 0)
+
+        def setup():
+            nc.vector.memset(one[:], 1.0)
+            nc.scalar.activation(out=one[:], in_=one[:], func=ACT.Sigmoid)
+
+        def scales(kind, queue):
+            for q in range(4):
+                p0 = 32 * q + first_row[kind]
+                engines[queue].dma_start(
+                    out=planes[kind][p0 : p0 + 4, :, :].bitcast(I32),
+                    in_=scale_rows[kind][:, 4 * q : 4 * q + 4, :].bitcast(I32).rearrange("g r n -> r g n"),
+                )
+            if queue == "G":
+                make_identity(nc, ident[:])
+
+        def load(kind, h, gs):
+            g = slice(gs[0], gs[-1] + 1)
+            if kind == "x":
+                src = x_words.rearrange("g p n t -> p g (n t)").bitcast(I32)
+                nc.sync.dma_start(out=x_codes[:, g, :], in_=src[:, g, :])
+            elif kind == "u":
+                src = u_words.rearrange("g p b -> p g b")[:, g, h * 2 * SPAN : (h + 1) * 2 * SPAN]
+                nc.sync.dma_start(out=u_codes[h][:, g, :].bitcast(I32), in_=src.bitcast(I32))
+            elif kind == "w":
+                src = w_words.rearrange("g p n t -> p g (n t)").bitcast(I32)
+                nc.sync.dma_start(out=w_codes[h][:, g, :], in_=src[:, g, cols(h)])
+            else:
+                src = r[gs[0] * SPAN : (gs[0] + 1) * SPAN, cols(h)].rearrange("(p t) n -> p t n", t=PACK)
+                nc.sync.dma_start(out=r_rows[h][:, gs[0], :, :], in_=src)
+
+        def part_of(part):
+            return (0, SPAN) if part is None else (part * SPAN // 2, (part + 1) * SPAN // 2)
+
+        def weave(h, g, engine, part=None):
+            a, b = part_of(part)
+            dst = r_woven[h][:, g, PACK * a : PACK * b].rearrange("p (c i t) -> p c t i", i=4, t=PACK)
+            src = r_rows[h][:, g, :, a:b].rearrange("p t (c i) -> p c t i", i=4)
+            if engine == "V":
+                nc.vector.tensor_copy(out=dst, in_=src)
+            else:
+                nc.scalar.copy(out=dst, in_=src)
+
+        def quant_r(h, g, part=None):
+            a, b = part_of(part)
+            nc.vector.quantize_mx(
+                out=r_codes[h][:, g, a:b].bitcast(FP8X4), scales=r_plane[h][:, g, a:b], in_=r_woven[h][:, g, PACK * a : PACK * b]
+            )
+
+        def mm(kind, h, j, g, b):
+            bank_of[kind, h, j] = banks[b]
+            if kind == "u":
+                rhs, rhs_scale = u_codes[h][:, g, :].bitcast(FP4X4), planes["u"][:, g, cols(h)]
+            elif kind == "w":
+                rhs, rhs_scale = w_codes[h][:, g, :].bitcast(FP8X4), planes["w"][W_ROW:P, g, cols(h)]
+            else:
+                rhs, rhs_scale = r_codes[h][:, g, :].bitcast(FP8X4), r_plane[h][:, g, :]
+            nc.tensor.matmul_mx(
+                out=banks[b][:],
+                lhsT=x_codes[:, g, rows(j)].bitcast(FP8X4),
+                lhsT_scale=planes["x"][:, g, rows(j)],
+                rhs=rhs,
+                rhs_scale=rhs_scale,
+                start=(g == 0),
+                stop=(g == PASSES - 1),
+            )
+
+        def keep_value(h, j):
+            kept.add((h, j))
+            nc.scalar.copy(out=y32[h][:, j, :], in_=bank_of["u", h, j][:])
+
+        def absolute(h, j):
+            nc.scalar.activation(out=gate[h][:, j, :], in_=bank_of["r", h, j][:], func=ACT.Abs)
+
+        def margin(h, j):
+            nc.vector.tensor_tensor(out=gate[h][:, j, :], in0=bank_of["w", h, j][:], in1=gate[h][:, j, :], op=ALU.subtract)
+
+        def sigmoid(h, j):
+            nc.scalar.activation(out=gate[h][:, j, :], in_=gate[h][:, j, :], func=ACT.Sigmoid)
+
+        def product(h, j):
+            value = y32[h][:, j, :] if (h, j) in kept else bank_of["u", h, j][:]
+            nc.vector.tensor_tensor(out=y32[h][:, j, :], in0=value, in1=gate[h][:, j, :], op=ALU.mult)
+
+        def by_pairs(ap):
+            return ap.rearrange("m (p u e) -> m u p e", u=2, e=2)
+
+        def pair_order(h, j):
+            return y16[h][:, j, :].rearrange("m (u p e) -> m u p e", u=2, e=2)
+
+        def product16(h, j):
+            nc.vector.tensor_tensor(
+                out=pair_order(h, j), in0=by_pairs(bank_of["u", h, j][:]), in1=by_pairs(gate[h][:, j, :]), op=ALU.mult
+            )
+
+        def round_y(h, j, engine):
+            if engine == "V":
+                nc.vector.tensor_copy(out=pair_order(h, j), in_=by_pairs(y32[h][:, j, :]))
+            else:
+                nc.scalar.copy(out=pair_order(h, j), in_=by_pairs(y32[h][:, j, :]))
+
+        def store_y(h, j):
+            nc.sync.dma_start(out=out_0[rows(j), cols(h)], in_=y32[h][:, j, :])
+
+        def turn(h, js, b):
+            bank_of["turn", h, js] = banks[b]
+            for i, j in enumerate(js):
+                pairs = y16[h][:, j, :].bitcast(F32)
+                for u in range(2):
+                    nc.tensor.transpose(banks[b][:, rows(2 * i + u)], pairs[:, rows(u)], ident[:])
+
+        def unload(h, js, engine):
+            width = len(js) * P
+            src = bank_of["turn", h, js][:, 0 : 2 * width].rearrange("p (i u m) -> p i m u", u=2, m=P)
+            dst = y_turned[h][:, js[0] * SPAN : (js[-1] + 1) * SPAN].bitcast(F32).rearrange("p (i m u) -> p i m u", u=2, m=P)
+            if engine == "V":
+                nc.vector.tensor_copy(out=dst, in_=src)
+            else:
+                nc.scalar.copy(out=dst, in_=src)
+
+        def quant_y(h, js):
+            samples = slice(js[0] * P, (js[-1] + 1) * P)
+            nc.vector.quantize_mx(
+                out=y_codes[h][:, samples].bitcast(FP8X4),
+                scales=y_plane[h][:, samples],
+                in_=y_turned[h][:, js[0] * SPAN : (js[-1] + 1) * SPAN],
+            )
+
+        def store_words(h, js):
+            samples = slice(js[0] * P, (js[-1] + 1) * P)
+            dst = out_1[h].rearrange("p m t -> p (m t)").bitcast(I32)
+            nc.sync.dma_start(out=dst[:, samples], in_=y_codes[h][:, samples])
+
+        def store_scales(h):
+            for q in range(4):
+                queue = nc.scalar if h == HALVES - 1 and q % 2 == 1 else nc.sync
+                queue.dma_start(
+                    out=out_2[h, 4 * q : 4 * q + 4, :].bitcast(I32), in_=y_plane[h][32 * q : 32 * q + 4, :].bitcast(I32)
+                )
+
+        run = {
+            "clear": clear, "setup": setup, "scales": scales, "load": load, "weave": weave, "quant_r": quant_r,
+            "mm": mm, "keep_value": keep_value, "absolute": absolute, "margin": margin, "sigmoid": sigmoid,
+            "product": product, "product16": product16, "round": round_y, "store_y": store_y, "turn": turn,
+            "unload": unload, "quant_y": quant_y, "store_words": store_words, "store_scales": store_scales,
+        }
+        with tc.manual_schedule():
+            for step in program_order():
+                run[step[0]](*step[1:])

@@ -23,6 +23,7 @@ TILES = M // P
 HALVES = N // SPAN
 BANKS = 8
 W_ROW = 4
+WARM_PASSES = 20
 
 
 def program_order():
@@ -37,24 +38,28 @@ def program_order():
         b = bank()
         steps.extend(("mm", kind, h, j, g, b) for g in range(PASSES))
 
-    steps += [("load", "x", 0, (0,)), ("load", "u", 0, (0,)), ("clear", "x", "V"), ("clear", "u", "V"), ("clear", "w", "G")]
-    steps += [("setup",), ("scales", "x", "D"), ("scales", "u", "D"), ("scales", "w", "G")]
+    steps += [("load", "x", 0, (0,), "G"), ("load", "u", 0, (0,)), ("clear", "x", "V"), ("clear", "u0", "V"), ("warm",)]
+    steps += [("scales", "x", "DDDD"), ("scales", "u0", "SSSS"), ("setup",), ("clear", "w", "G"), ("scales", "w", "GGGG")]
+    steps += [("identity",), ("clear", "u1", "V")]
     steps += [("load", "x", 0, (1,)), ("load", "u", 0, (1, 2)), ("load", "r", 0, (0,)), ("load", "x", 0, (2,))]
     steps += [("load", "r", 0, (1,)), ("load", "r", 0, (2,)), ("load", "r", 1, (0,)), ("load", "r", 1, (1,))]
     steps += [("load", "w", 0, (0, 1, 2)), ("load", "r", 1, (2,)), ("load", "w", 1, (0, 1, 2)), ("load", "u", 1, (0, 1, 2))]
+    steps += [("scales", "u1", "DDDD")]
 
     banks = [bank() for j in range(TILES)]
     for g in range(PASSES):
         steps.extend(("mm", "u", 0, j, g, banks[j]) for j in range(TILES))
-    steps.extend(("keep_value", 0, j) for j in range(TILES))
+    steps.extend(("keep_value", 0, j) for j in range(4))
     for g in range(PASSES):
-        steps += [("weave", 0, g, "V", 0), ("weave", 0, g, "V", 1), ("quant_r", 0, g, 0), ("quant_r", 0, g, 1)]
-    steps += [("weave", 1, 0, "S")]
+        second = "S" if g == 2 else "V"
+        steps += [("weave", 0, g, "V", 0), ("weave", 0, g, second, 1), ("quant_r", 0, g, 0), ("quant_r", 0, g, 1)]
+    steps.extend(("keep_value", 0, j) for j in range(4, TILES))
+    steps += [("weave", 1, 0, "V"), ("weave", 1, 1, "V")]
     banks = [bank() for j in range(TILES)]
     for g in range(PASSES):
         steps.extend(("mm", "r", 0, j, g, banks[j]) for j in range(TILES))
     steps.extend(("absolute", 0, j) for j in range(TILES))
-    steps += [("weave", 1, 1, "V"), ("quant_r", 1, 0), ("quant_r", 1, 1), ("weave", 1, 2, "V")]
+    steps += [("quant_r", 1, 0), ("quant_r", 1, 1), ("weave", 1, 2, "S", 1)]
     for j in range(TILES):
         group("w", 0, j)
 
@@ -82,9 +87,10 @@ def program_order():
         add("store_words", h, js)
 
     gate(0, 0)
-    add("quant_r", 1, 2)
+    add("weave", 1, 2, "V", 0)
     gate(0, 1)
     gate(0, 2)
+    add("quant_r", 1, 2)
     product(0, 0)
     gate(0, 3)
     product(0, 1)
@@ -170,7 +176,8 @@ def tile_virtual_logit_gated_features_k3_kernel(
         r_woven = [sb("r_woven%d" % h, [P, PASSES, SPAN * PACK], BF16) for h in range(HALVES)]
         planes = {
             "x": sb("x_plane", [P, PASSES, M], U8),
-            "u": sb("u_plane", [P, PASSES, N], U8),
+            "u0": sb("u_plane0", [P, PASSES, SPAN], U8),
+            "u1": sb("u_plane1", [P, PASSES, SPAN], U8),
             "w": sb("w_plane", [P, PASSES, N], U8),
         }
         gate = [sb("gate%d" % h, [P, TILES, SPAN], F32) for h in range(HALVES)]
@@ -181,8 +188,11 @@ def tile_virtual_logit_gated_features_k3_kernel(
         y_plane = [sb("y_plane%d" % h, [P, M], U8) for h in range(HALVES)]
         ident = sb("ident", [P, P], F32)
         one = sb("one", [P, 1], F32)
-        scale_rows = {"x": x_scales, "u": u_scales, "w": w_scales}
-        first_row = {"x": 0, "u": 0, "w": W_ROW}
+        idle = sb("idle", [P, SPAN], BF16)
+        idle_codes = sb("idle_codes", [P, P], I32)
+        idle_plane = sb("idle_plane", [P, P], U8)
+        scale_rows = {"x": x_scales, "u0": u_scales[:, :, 0:SPAN], "u1": u_scales[:, :, SPAN:N], "w": w_scales}
+        first_row = {"x": 0, "u0": 0, "u1": 0, "w": W_ROW}
         bank_of = {}
         kept = set()
 
@@ -199,21 +209,36 @@ def tile_virtual_logit_gated_features_k3_kernel(
             nc.vector.memset(one[:], 1.0)
             nc.scalar.activation(out=one[:], in_=one[:], func=ACT.Sigmoid)
 
-        def scales(kind, queue):
+        def warm():
+            nc.vector.memset(idle[:], 1.0)
+            nc.vector.quantize_mx(out=idle_codes[:].bitcast(FP8X4), scales=idle_plane[:], in_=idle[:])
+            for i in range(WARM_PASSES):
+                nc.tensor.matmul_mx(
+                    out=banks[BANKS - 1][:, rows(i % 4)],
+                    lhsT=idle_codes[:].bitcast(FP8X4),
+                    lhsT_scale=idle_plane[:],
+                    rhs=idle_codes[:].bitcast(FP8X4),
+                    rhs_scale=idle_plane[:],
+                    start=True,
+                    stop=True,
+                )
+
+        def identity():
+            make_identity(nc, ident[:])
+
+        def scales(kind, queues):
             for q in range(4):
                 p0 = 32 * q + first_row[kind]
-                engines[queue].dma_start(
+                engines[queues[q]].dma_start(
                     out=planes[kind][p0 : p0 + 4, :, :].bitcast(I32),
                     in_=scale_rows[kind][:, 4 * q : 4 * q + 4, :].bitcast(I32).rearrange("g r n -> r g n"),
                 )
-            if queue == "G":
-                make_identity(nc, ident[:])
 
-        def load(kind, h, gs):
+        def load(kind, h, gs, queue="D"):
             g = slice(gs[0], gs[-1] + 1)
             if kind == "x":
                 src = x_words.rearrange("g p n t -> p g (n t)").bitcast(I32)
-                nc.sync.dma_start(out=x_codes[:, g, :], in_=src[:, g, :])
+                engines[queue].dma_start(out=x_codes[:, g, :], in_=src[:, g, :])
             elif kind == "u":
                 src = u_words.rearrange("g p b -> p g b")[:, g, h * 2 * SPAN : (h + 1) * 2 * SPAN]
                 nc.sync.dma_start(out=u_codes[h][:, g, :].bitcast(I32), in_=src.bitcast(I32))
@@ -245,7 +270,7 @@ def tile_virtual_logit_gated_features_k3_kernel(
         def mm(kind, h, j, g, b):
             bank_of[kind, h, j] = banks[b]
             if kind == "u":
-                rhs, rhs_scale = u_codes[h][:, g, :].bitcast(FP4X4), planes["u"][:, g, cols(h)]
+                rhs, rhs_scale = u_codes[h][:, g, :].bitcast(FP4X4), planes["u%d" % h][:, g, :]
             elif kind == "w":
                 rhs, rhs_scale = w_codes[h][:, g, :].bitcast(FP8X4), planes["w"][W_ROW:P, g, cols(h)]
             else:
@@ -334,7 +359,7 @@ def tile_virtual_logit_gated_features_k3_kernel(
                 )
 
         run = {
-            "clear": clear, "setup": setup, "scales": scales, "load": load, "weave": weave, "quant_r": quant_r,
+            "warm": warm, "identity": identity, "clear": clear, "setup": setup, "scales": scales, "load": load, "weave": weave, "quant_r": quant_r,
             "mm": mm, "keep_value": keep_value, "absolute": absolute, "margin": margin, "sigmoid": sigmoid,
             "product": product, "product16": product16, "round": round_y, "store_y": store_y, "turn": turn,
             "unload": unload, "quant_y": quant_y, "store_words": store_words, "store_scales": store_scales,

from contextlib import ExitStack

import concourse.mybir as mybir
from concourse.masks import make_identity

M, K, N = 768, 1536, 1024
FLOPS = 3 * 2 * M * K * N

F32 = mybir.dt.float32
BF16 = mybir.dt.bfloat16
I32 = mybir.dt.int32
U8 = mybir.dt.uint8
FP8X4 = mybir.dt.float8_e4m3fn_x4
FP4X4 = mybir.dt.float4_e2m1fn_x4
ACT = mybir.ActivationFunctionType
ALU = mybir.AluOpType

P = 128
PACK = 4
SPAN = P * PACK
PASSES = K // SPAN
TILES = M // P
HALVES = N // SPAN
BANKS = 8
W_ROW = 4
WARM_PASSES = 20


def program_order():
    steps = []
    used = [0]

    def bank():
        used[0] += 1
        return (used[0] - 1) % 8

    def group(kind, h, j):
        b = bank()
        steps.extend(("mm", kind, h, j, g, b) for g in range(PASSES))

    steps += [("load", "x", 0, (0,), "G"), ("load", "u", 0, (0,)), ("clear", "x", "V"), ("clear", "u0", "V"), ("warm",)]
    steps += [("scales", "x", "DDDD"), ("scales", "u0", "SSSS"), ("setup",), ("clear", "w", "G"), ("scales", "w", "GGGG")]
    steps += [("identity",), ("clear", "u1", "V")]
    steps += [("load", "x", 0, (1,)), ("load", "u", 0, (1, 2)), ("load", "r", 0, (0,)), ("load", "x", 0, (2,))]
    steps += [("load", "r", 0, (1,)), ("load", "r", 0, (2,)), ("load", "r", 1, (0,)), ("load", "r", 1, (1,))]
    steps += [("load", "w", 0, (0, 1, 2)), ("load", "r", 1, (2,)), ("load", "w", 1, (0, 1, 2)), ("load", "u", 1, (0, 1, 2))]
    steps += [("scales", "u1", "DDDD")]

    banks = [bank() for j in range(TILES)]
    for g in range(PASSES):
        steps.extend(("mm", "u", 0, j, g, banks[j]) for j in range(TILES))
    steps.extend(("keep_value", 0, j) for j in range(4))
    for g in range(PASSES):
        second = "S" if g == 2 else "V"
        steps += [("weave", 0, g, "V", 0), ("weave", 0, g, second, 1), ("quant_r", 0, g, 0), ("quant_r", 0, g, 1)]
    steps.extend(("keep_value", 0, j) for j in range(4, TILES))
    steps += [("weave", 1, 0, "V"), ("weave", 1, 1, "V")]
    banks = [bank() for j in range(TILES)]
    for g in range(PASSES):
        steps.extend(("mm", "r", 0, j, g, banks[j]) for j in range(TILES))
    steps.extend(("absolute", 0, j) for j in range(TILES))
    steps += [("quant_r", 1, 0), ("quant_r", 1, 1), ("weave", 1, 2, "S", 1)]
    for j in range(TILES):
        group("w", 0, j)

    def turn(*pairs):
        steps.extend(("turn", h, js, bank()) for h, js in pairs)

    def finish(h, js):
        steps.extend([("unload", h, js, "S"), ("quant_y", h, js), ("store_words", h, js)])

    def gate(h, j):
        steps.extend([("margin", h, j), ("sigmoid", h, j)])

    def result(h, j, engine):
        steps.extend([("product", h, j), ("store_y", h, j), ("round", h, j, engine)])

    def add(name, *args):
        steps.append((name,) + args)

    def product(h, j):
        add("product", h, j)
        add("store_y", h, j)

    def planes(h, js):
        add("quant_y", h, js)
        add("store_words", h, js)

    gate(0, 0)
    add("weave", 1, 2, "V", 0)
    gate(0, 1)
    gate(0, 2)
    add("quant_r", 1, 2)
    product(0, 0)
    gate(0, 3)
    product(0, 1)
    add("round", 0, 0, "S")
    scalar_fill = {
        0: [("sigmoid", 0, 4), ("sigmoid", 0, 5)],
        1: [("round", 0, 2, "S")],
        2: [("round", 0, 4, "S")],
        3: [("unload", 0, (0, 1), "S"), ("unload", 0, (2, 3), "S")],
        4: [("unload", 0, (4, 5), "S"), ("unload", 1, (0, 1), "S")],
        5: [],
    }
    add("margin", 0, 4)
    add("margin", 0, 5)
    add("round", 0, 1, "V")
    for j in range(TILES):
        group("r", 1, j)
        add("absolute", 1, j)
        steps.extend(scalar_fill[j])
        group("w", 1, j)
        gate(1, j)
        if j == 1:
            add("round", 0, 3, "V")
        if j > 0:
            group("u", 1, j - 1)
            product(1, j - 1)
        if j == 0:
            product(0, 2)
        if j < 3:
            product(0, j + 3)
        if j == 3:
            planes(0, (0, 1))
        if j == 4:
            planes(0, (4, 5))
            add("store_scales", 0)
        if 0 < j < 5:
            add("round", 1, j - 1, "V")
        if j == 2:
            add("round", 0, 5, "V")
        if j == 3:
            planes(0, (2, 3))
        if j == 4:
            planes(1, (0, 1))
        if j == 2:
            turn((0, (0, 1)), (0, (2, 3)))
        if j == 3:
            turn((0, (4, 5)), (1, (0, 1)))
    add("round", 1, 4, "S")
    group("u", 1, 5)
    add("product16", 1, 5)
    product(1, 5)
    turn((1, (2, 3)), (1, (4,)), (1, (5,)))
    finish(1, (2, 3))
    add("unload", 1, (4,), "S")
    add("unload", 1, (5,), "V")
    add("quant_y", 1, (4,))
    add("quant_y", 1, (5,))
    add("store_words", 1, (4, 5))
    add("store_scales", 1)
    return steps


def tile_virtual_logit_gated_features_k3_kernel(
    tc, x_words, x_scales, u_words, u_scales, w_words, w_scales, r, out_0, out_1, out_2
):
    nc = tc.nc
    engines = {"V": nc.vector, "S": nc.scalar, "G": nc.gpsimd, "D": nc.sync}

    with ExitStack() as ctx:
        keep = ctx.enter_context(tc.tile_pool(name="keep", bufs=1))
        psum = ctx.enter_context(tc.psum_pool(name="psum", bufs=1))

        def sb(name, shape, dtype):
            return keep.tile(shape, dtype, name=name, align_bytes=64)

        banks = [psum.tile([P, SPAN], F32, name="bank%d" % b) for b in range(BANKS)]
        x_codes = sb("x_codes", [P, PASSES, M], I32)
        u_codes = [sb("u_codes%d" % h, [P, PASSES, 2 * SPAN], U8) for h in range(HALVES)]
        w_codes = [sb("w_codes%d" % h, [P, PASSES, SPAN], I32) for h in range(HALVES)]
        r_codes = [sb("r_codes%d" % h, [P, PASSES, SPAN], I32) for h in range(HALVES)]
        r_plane = [sb("r_plane%d" % h, [P, PASSES, SPAN], U8) for h in range(HALVES)]
        r_rows = [sb("r_rows%d" % h, [P, PASSES, PACK, SPAN], BF16) for h in range(HALVES)]
        r_woven = [sb("r_woven%d" % h, [P, PASSES, SPAN * PACK], BF16) for h in range(HALVES)]
        planes = {
            "x": sb("x_plane", [P, PASSES, M], U8),
            "u0": sb("u_plane0", [P, PASSES, SPAN], U8),
            "u1": sb("u_plane1", [P, PASSES, SPAN], U8),
            "w": sb("w_plane", [P, PASSES, N], U8),
        }
        gate = [sb("gate%d" % h, [P, TILES, SPAN], F32) for h in range(HALVES)]
        y32 = [sb("y32_%d" % h, [P, TILES, SPAN], F32) for h in range(HALVES)]
        y16 = [sb("y16_%d" % h, [P, TILES, SPAN], BF16) for h in range(HALVES)]
        y_turned = [sb("y_turned%d" % h, [P, M * PACK], BF16) for h in range(HALVES)]
        y_codes = [sb("y_codes%d" % h, [P, M], I32) for h in range(HALVES)]
        y_plane = [sb("y_plane%d" % h, [P, M], U8) for h in range(HALVES)]
        ident = sb("ident", [P, P], F32)
        one = sb("one", [P, 1], F32)
        idle = sb("idle", [P, SPAN], BF16)
        idle_codes = sb("idle_codes", [P, P], I32)
        idle_plane = sb("idle_plane", [P, P], U8)
        scale_rows = {"x": x_scales, "u0": u_scales[:, :, 0:SPAN], "u1": u_scales[:, :, SPAN:N], "w": w_scales}
        first_row = {"x": 0, "u0": 0, "u1": 0, "w": W_ROW}
        bank_of = {}
        kept = set()

        def cols(h):
            return slice(h * SPAN, (h + 1) * SPAN)

        def rows(j):
            return slice(j * P, (j + 1) * P)

        def clear(kind, engine):
            engines[engine].memset(planes[kind][:].rearrange("p g n -> p (g n)").bitcast(I32), 0)

        def setup():
            nc.vector.memset(one[:], 1.0)
            nc.scalar.activation(out=one[:], in_=one[:], func=ACT.Sigmoid)

        def warm():
            nc.vector.memset(idle[:], 1.0)
            nc.vector.quantize_mx(out=idle_codes[:].bitcast(FP8X4), scales=idle_plane[:], in_=idle[:])
            for i in range(WARM_PASSES):
                nc.tensor.matmul_mx(
                    out=banks[BANKS - 1][:, rows(i % 4)],
                    lhsT=idle_codes[:].bitcast(FP8X4),
                    lhsT_scale=idle_plane[:],
                    rhs=idle_codes[:].bitcast(FP8X4),
                    rhs_scale=idle_plane[:],
                    start=True,
                    stop=True,
                )

        def identity():
            make_identity(nc, ident[:])

        def scales(kind, queues):
            for q in range(4):
                p0 = 32 * q + first_row[kind]
                engines[queues[q]].dma_start(
                    out=planes[kind][p0 : p0 + 4, :, :].bitcast(I32),
                    in_=scale_rows[kind][:, 4 * q : 4 * q + 4, :].bitcast(I32).rearrange("g r n -> r g n"),
                )

        def load(kind, h, gs, queue="D"):
            g = slice(gs[0], gs[-1] + 1)
            if kind == "x":
                src = x_words.rearrange("g p n t -> p g (n t)").bitcast(I32)
                engines[queue].dma_start(out=x_codes[:, g, :], in_=src[:, g, :])
            elif kind == "u":
                src = u_words.rearrange("g p b -> p g b")[:, g, h * 2 * SPAN : (h + 1) * 2 * SPAN]
                nc.sync.dma_start(out=u_codes[h][:, g, :].bitcast(I32), in_=src.bitcast(I32))
            elif kind == "w":
                src = w_words.rearrange("g p n t -> p g (n t)").bitcast(I32)
                nc.sync.dma_start(out=w_codes[h][:, g, :], in_=src[:, g, cols(h)])
            else:
                src = r[gs[0] * SPAN : (gs[0] + 1) * SPAN, cols(h)].rearrange("(p t) n -> p t n", t=PACK)
                nc.sync.dma_start(out=r_rows[h][:, gs[0], :, :], in_=src)

        def part_of(part):
            return (0, SPAN) if part is None else (part * SPAN // 2, (part + 1) * SPAN // 2)

        def weave(h, g, engine, part=None):
            a, b = part_of(part)
            dst = r_woven[h][:, g, PACK * a : PACK * b].rearrange("p (c i t) -> p c t i", i=4, t=PACK)
            src = r_rows[h][:, g, :, a:b].rearrange("p t (c i) -> p c t i", i=4)
            if engine == "V":
                nc.vector.tensor_copy(out=dst, in_=src)
            else:
                nc.scalar.copy(out=dst, in_=src)

        def quant_r(h, g, part=None):
            a, b = part_of(part)
            nc.vector.quantize_mx(
                out=r_codes[h][:, g, a:b].bitcast(FP8X4), scales=r_plane[h][:, g, a:b], in_=r_woven[h][:, g, PACK * a : PACK * b]
            )

        def mm(kind, h, j, g, b):
            bank_of[kind, h, j] = banks[b]
            if kind == "u":
                rhs, rhs_scale = u_codes[h][:, g, :].bitcast(FP4X4), planes["u%d" % h][:, g, :]
            elif kind == "w":
                rhs, rhs_scale = w_codes[h][:, g, :].bitcast(FP8X4), planes["w"][W_ROW:P, g, cols(h)]
            else:
                rhs, rhs_scale = r_codes[h][:, g, :].bitcast(FP8X4), r_plane[h][:, g, :]
            nc.tensor.matmul_mx(
                out=banks[b][:],
                lhsT=x_codes[:, g, rows(j)].bitcast(FP8X4),
                lhsT_scale=planes["x"][:, g, rows(j)],
                rhs=rhs,
                rhs_scale=rhs_scale,
                start=(g == 0),
                stop=(g == PASSES - 1),
            )

        def keep_value(h, j):
            kept.add((h, j))
            nc.scalar.copy(out=y32[h][:, j, :], in_=bank_of["u", h, j][:])

        def absolute(h, j):
            nc.scalar.activation(out=gate[h][:, j, :], in_=bank_of["r", h, j][:], func=ACT.Abs)

        def margin(h, j):
            nc.vector.tensor_tensor(out=gate[h][:, j, :], in0=bank_of["w", h, j][:], in1=gate[h][:, j, :], op=ALU.subtract)

        def sigmoid(h, j):
            nc.scalar.activation(out=gate[h][:, j, :], in_=gate[h][:, j, :], func=ACT.Sigmoid)

        def product(h, j):
            value = y32[h][:, j, :] if (h, j) in kept else bank_of["u", h, j][:]
            nc.vector.tensor_tensor(out=y32[h][:, j, :], in0=value, in1=gate[h][:, j, :], op=ALU.mult)

        def by_pairs(ap):
            return ap.rearrange("m (p u e) -> m u p e", u=2, e=2)

        def pair_order(h, j):
            return y16[h][:, j, :].rearrange("m (u p e) -> m u p e", u=2, e=2)

        def product16(h, j):
            nc.vector.tensor_tensor(
                out=pair_order(h, j), in0=by_pairs(bank_of["u", h, j][:]), in1=by_pairs(gate[h][:, j, :]), op=ALU.mult
            )

        def round_y(h, j, engine):
            if engine == "V":
                nc.vector.tensor_copy(out=pair_order(h, j), in_=by_pairs(y32[h][:, j, :]))
            else:
                nc.scalar.copy(out=pair_order(h, j), in_=by_pairs(y32[h][:, j, :]))

        def store_y(h, j):
            nc.sync.dma_start(out=out_0[rows(j), cols(h)], in_=y32[h][:, j, :])

        def turn(h, js, b):
            bank_of["turn", h, js] = banks[b]
            for i, j in enumerate(js):
                pairs = y16[h][:, j, :].bitcast(F32)
                for u in range(2):
                    nc.tensor.transpose(banks[b][:, rows(2 * i + u)], pairs[:, rows(u)], ident[:])

        def unload(h, js, engine):
            width = len(js) * P
            src = bank_of["turn", h, js][:, 0 : 2 * width].rearrange("p (i u m) -> p i m u", u=2, m=P)
            dst = y_turned[h][:, js[0] * SPAN : (js[-1] + 1) * SPAN].bitcast(F32).rearrange("p (i m u) -> p i m u", u=2, m=P)
            if engine == "V":
                nc.vector.tensor_copy(out=dst, in_=src)
            else:
                nc.scalar.copy(out=dst, in_=src)

        def quant_y(h, js):
            samples = slice(js[0] * P, (js[-1] + 1) * P)
            nc.vector.quantize_mx(
                out=y_codes[h][:, samples].bitcast(FP8X4),
                scales=y_plane[h][:, samples],
                in_=y_turned[h][:, js[0] * SPAN : (js[-1] + 1) * SPAN],
            )

        def store_words(h, js):
            samples = slice(js[0] * P, (js[-1] + 1) * P)
            dst = out_1[h].rearrange("p m t -> p (m t)").bitcast(I32)
            nc.sync.dma_start(out=dst[:, samples], in_=y_codes[h][:, samples])

        def store_scales(h):
            for q in range(4):
                queue = nc.scalar if h == HALVES - 1 and q % 2 == 1 else nc.sync
                queue.dma_start(
                    out=out_2[h, 4 * q : 4 * q + 4, :].bitcast(I32), in_=y_plane[h][32 * q : 32 * q + 4, :].bitcast(I32)
                )

        run = {
            "warm": warm, "identity": identity, "clear": clear, "setup": setup, "scales": scales, "load": load, "weave": weave, "quant_r": quant_r,
            "mm": mm, "keep_value": keep_value, "absolute": absolute, "margin": margin, "sigmoid": sigmoid,
            "product": product, "product16": product16, "round": round_y, "store_y": store_y, "turn": turn,
            "unload": unload, "quant_y": quant_y, "store_words": store_words, "store_scales": store_scales,
        }
        with tc.manual_schedule():
            for step in program_order():
                run[step[0]](*step[1:])
